import numpy as np
import ml_dtypes


def mxq(x, axis, fmt="e4m3"):
    dtype, down = {"e4m3": (ml_dtypes.float8_e4m3fn, 7), "e5m2": (ml_dtypes.float8_e5m2, 14)}[fmt]
    v = np.moveaxis(np.asarray(x, np.float32).astype(ml_dtypes.bfloat16).astype(np.float64), axis, -1)
    blocks = v.reshape(v.shape[:-1] + (-1, 32))
    amax = np.abs(blocks).max(-1, keepdims=True)
    byte = np.maximum(np.where(amax > 0, np.frexp(amax)[1] - 1 + 127, 0) - down, 1)
    scale = np.exp2(byte - 127.0)
    codes = (blocks / scale).astype(np.float32).astype(dtype).astype(np.float64)
    return np.moveaxis((codes * scale).reshape(v.shape), -1, axis)


WIDE = False


def mx_kscale(k):
    if not WIDE:
        return np.ones(k)
    levels = np.array([10, -10, 5, -5, 0])
    if k % 512:
        return np.exp2(np.random.permutation(np.resize(levels, k // 32))).repeat(32)
    a = np.empty((k // 512, 16))
    for p in range(k // 512):
        a[p, :8] = np.random.permutation(np.resize(levels, 8))
        for g in range(8):
            far = levels[np.abs(levels - a[p, g]) >= 10]
            a[p, g + 8] = far[np.random.randint(len(far))]
    return np.exp2(a.ravel()).repeat(32)


def f64(x):
    return np.asarray(x).astype(np.float64)


E2M1 = np.array([0.0, 0.5, 1.0, 1.5, 2.0, 3.0, 4.0, 6.0, -0.0, -0.5, -1.0, -1.5, -2.0, -3.0, -4.0, -6.0])


def pack_weight(w, fmt):
    k, n = w.shape
    w = f64(np.asarray(w, np.float32).astype(ml_dtypes.bfloat16)).reshape(k // 32, 32, n)
    amax = np.abs(w).max(1)
    if fmt == "e4m3":
        byte = np.frexp(amax)[1] - 1 + 127 - 7
    else:
        mant, ex = np.frexp(amax / 6.0)
        byte = np.where(mant > 0.5, ex, ex - 1) + 127
    byte = np.clip(np.where(amax > 0, byte, 1), 1, 254)
    scaled = (w * np.exp2(127.0 - byte)[:, None, :]).reshape(k, n).astype(np.float32)
    by_word = np.ascontiguousarray(scaled.reshape(k // 512, 128, 4, n).transpose(0, 1, 3, 2))
    if fmt == "e4m3":
        words = by_word.astype(ml_dtypes.float8_e4m3fn).view(np.uint8)
    else:
        c = by_word.astype(ml_dtypes.float4_e2m1fn).view(np.uint8) & 0xF
        words = (c[..., 0::2] | (c[..., 1::2] << 4)).reshape(k // 512, 128, 2 * n)
    return np.ascontiguousarray(words), np.ascontiguousarray(byte.astype(np.uint8).reshape(k // 512, 16, n))


def unpack_weight(words, scales, fmt):
    g, _, n = scales.shape
    words = np.ascontiguousarray(words).reshape(g, 128, n, -1)
    if fmt == "e4m3":
        vals = words.view(ml_dtypes.float8_e4m3fn).astype(np.float64)
    else:
        nib = np.empty((g, 128, n, 4), np.uint8)
        nib[..., 0::2] = words & 0xF
        nib[..., 1::2] = words >> 4
        vals = E2M1[nib]
    vals = vals * np.repeat(np.exp2(scales.astype(np.float64) - 127.0), 8, axis=1)[..., None]
    return vals.transpose(0, 1, 3, 2).reshape(g * 512, n)


D, K, M, T = 256, 1536, 1024, 1024


def setup_inputs():
    n = np.random.standard_normal
    s = mx_kscale(K)[:, None]
    p_w0 = pack_weight(n((K, M)) / np.sqrt(K) / s, "e2m1")
    p_w1 = pack_weight(n((K, M)) / np.sqrt(K) / s, "e4m3")
    return {
        "x": (n((K, T + 2 * D)) * s).astype(np.float32),
        "w0_words": p_w0[0],
        "w0_scales": p_w0[1],
        "w1_words": p_w1[0],
        "w1_scales": p_w1[1],
        "w2": (n((K, M)) / np.sqrt(K) / s).astype(np.float32),
        "r": (n((1024, 1024))).astype(np.float32),
    }


def reference(x, w0_words, w0_scales, w1_words, w1_scales, w2, r):
    x_ = mxq(f64(x), 0, "e4m3")
    w0_ = unpack_weight(w0_words, w0_scales, "e2m1")
    w1_ = unpack_weight(w1_words, w1_scales, "e4m3")
    w2_ = mxq(f64(w2), 0, "e4m3")
    y = x_[:, :T].T @ w0_ + x_[:, D:D + T].T @ w1_ + x_[:, 2 * D:].T @ w2_
    return f64(r) + y

@@ -1,0 +1,258 @@
+from contextlib import ExitStack
+
+import concourse.mybir as mybir
+
+D, K, M, T = 256, 1536, 1024, 1024
+FLOPS = 2 * 3 * K * M * T
+
+F32 = mybir.dt.float32
+BF16 = mybir.dt.bfloat16
+I32 = mybir.dt.int32
+U32 = mybir.dt.uint32
+U8 = mybir.dt.uint8
+FP8X4 = mybir.dt.float8_e4m3fn_x4
+FP4X4 = mybir.dt.float4_e2m1fn_x4
+ADD = mybir.AluOpType.add
+
+P = 128
+PACK = 4
+K_PASS = P * PACK
+PASSES = K // K_PASS
+CHUNK = D
+N_TILE = 512
+X_COLS = T + 2 * D
+EARLY_CHUNKS = 4
+BANKS = [(0, 0), (1, 0), (0, 1), (1, 1)]
+
+
+def tile_mix_dconv_tm_res_kernel(tc, x, w0_words, w0_scales, w1_words, w1_scales, w2, r, out):
+    nc = tc.nc
+    with ExitStack() as ctx:
+        keep = ctx.enter_context(tc.tile_pool(name="keep", bufs=1))
+        raw_pool = ctx.enter_context(tc.tile_pool(name="raw", bufs=6))
+        stage = ctx.enter_context(tc.tile_pool(name="stage", bufs=6))
+        psum = ctx.enter_context(tc.psum_pool(name="psum", bufs=1))
+        ctx.enter_context(tc.manual_schedule())
+
+        x_codes = [keep.tile([P, X_COLS], U32, name="x_codes%d" % a, align_bytes=256) for a in range(PASSES)]
+        x_scales = [keep.tile([P, X_COLS], U8, name="x_scales%d" % a, align_bytes=256) for a in range(PASSES)]
+        w2_codes = [keep.tile([P, M], U32, name="w2_codes%d" % a, align_bytes=256) for a in range(PASSES)]
+        w2_scales = [keep.tile([P, M], U8, name="w2_scales%d" % a, align_bytes=256) for a in range(PASSES)]
+        w0_codes = keep.tile([P, PASSES * 2 * M], U8, align_bytes=256)
+        w0_plane = keep.tile([P, PASSES * M], U8, align_bytes=256)
+        w1_first = keep.tile([P, M], U32, align_bytes=256)
+        w1_rest = keep.tile([P, (PASSES - 1) * M], U32, align_bytes=256)
+        w1_plane = keep.tile([P, M], U8, align_bytes=256)
+        res = [keep.tile([P, 2 * M], F32, name="res%d" % j) for j in range(4)]
+        partial = [keep.tile([P, 2 * M], F32, name="partial%d" % j) for j in range(2)]
+
+        x_raw = {}
+        w2_raw = {}
+        staged = {}
+        acc = {}
+
+        def load_x(a, c0, c1):
+            raw = raw_pool.tile([P, PACK, (c1 - c0) * CHUNK], F32, name="raw", tag="raw")
+            rows = x[a * K_PASS : (a + 1) * K_PASS, c0 * CHUNK : c1 * CHUNK]
+            nc.sync.dma_start(out=raw[:], in_=rows.rearrange("(p i) w -> p i w", i=PACK))
+            for c in range(c0, c1):
+                x_raw[(a, c)] = raw[:, :, (c - c0) * CHUNK : (c - c0 + 1) * CHUNK]
+
+        def load_w2(a):
+            raw = raw_pool.tile([P, PACK, M], F32, name="raw", tag="raw")
+            rows = w2[a * K_PASS : (a + 1) * K_PASS, :]
+            nc.sync.dma_start(out=raw[:], in_=rows.rearrange("(p i) w -> p i w", i=PACK))
+            for c in range(M // CHUNK):
+                w2_raw[(a, c)] = raw[:, :, c * CHUNK : (c + 1) * CHUNK]
+
+        def copy_on(engine, dst, src):
+            if engine == "vector":
+                nc.vector.tensor_copy(out=dst, in_=src)
+            else:
+                nc.scalar.copy(out=dst, in_=src)
+
+        def round_x(engine, a, c):
+            grouped = stage.tile([P, PACK * CHUNK], BF16, name="grouped", tag="grouped", align_bytes=256)
+            copy_on(
+                engine,
+                grouped[:].rearrange("p (u g e i) -> p g i u e", u=2, e=2, i=PACK),
+                x_raw[(a, c)].rearrange("p i (g e u) -> p g i u e", e=2, u=2),
+            )
+            staged[("x", a, c)] = grouped
+
+        def round_w2(engine, a, c):
+            grouped = stage.tile([P, PACK * CHUNK], BF16, name="grouped", tag="grouped", align_bytes=256)
+            copy_on(
+                engine,
+                grouped[:].rearrange("p (g e i) -> p g i e", e=4, i=PACK),
+                w2_raw[(a, c)].rearrange("p i (g e) -> p g i e", e=4),
+            )
+            staged[("w2", a, c)] = grouped
+
+        def quantize(name, a, c):
+            codes, scales = (x_codes, x_scales) if name == "x" else (w2_codes, w2_scales)
+            cols = slice(c * CHUNK, (c + 1) * CHUNK)
+            nc.vector.quantize_mx(
+                out=codes[a][:, cols].bitcast(FP8X4), scales=scales[a][:, cols], in_=staged[(name, a, c)][:]
+            )
+
+        def open_banks(j, first_bank):
+            for b, (u, h) in enumerate(BANKS):
+                tag = "bank%d" % (first_bank + b)
+                acc[(j, u, h)] = psum.tile([P, N_TILE], F32, name=tag, tag=tag)
+
+        def mm(j, u, h, tap, a, start=False, stop=False):
+            t0 = (j + tap) * CHUNK + u * P
+            n0 = h * N_TILE
+            if tap == 0:
+                rhs = w0_codes[:, 2 * (a * M + n0) : 2 * (a * M + n0 + N_TILE)].bitcast(FP4X4)
+                rhs_scale = w0_plane[:, a * M + n0 : a * M + n0 + N_TILE]
+            elif tap == 1:
+                words = w1_first[:, n0 : n0 + N_TILE] if a == 0 else w1_rest[:, (a - 1) * M + n0 : (a - 1) * M + n0 + N_TILE]
+                rhs = words.bitcast(FP8X4)
+                rhs_scale = w1_plane[4 * (a + 1) : P, n0 : n0 + N_TILE]
+            else:
+                rhs = w2_codes[a][:, n0 : n0 + N_TILE].bitcast(FP8X4)
+                rhs_scale = w2_scales[a][:, n0 : n0 + N_TILE]
+            nc.tensor.matmul_mx(
+                out=acc[(j, u, h)][:],
+                lhsT=x_codes[a][:, t0 : t0 + P].bitcast(FP8X4),
+                lhsT_scale=x_scales[a][:, t0 : t0 + P],
+                rhs=rhs,
+                rhs_scale=rhs_scale,
+                start=start,
+                stop=stop,
+            )
+
+        def mm_block(j, tap, a, start=False, stop=False):
+            for u, h in BANKS:
+                mm(j, u, h, tap, a, start, stop)
+
+        def mm_bank(j, u, h, taps, start=False, stop=False):
+            steps = [(tap, a) for tap in taps for a in range(PASSES)]
+            for s, (tap, a) in enumerate(steps):
+                mm(j, u, h, tap, a, start and s == 0, stop and s == len(steps) - 1)
+
+        def cols_of(u, h):
+            return slice(u * M + h * N_TILE, u * M + (h + 1) * N_TILE)
+
+        def park(j, u, h):
+            nc.scalar.copy(out=partial[j][:, cols_of(u, h)], in_=acc[(j, u, h)][:])
+
+        def add_bank(dst, j, u, h):
+            view = dst[:, cols_of(u, h)]
+            nc.vector.tensor_tensor(out=view, in0=acc[(j, u, h)][:], in1=view, op=ADD)
+
+        def rows_of(dram, j):
+            return dram[j * CHUNK : (j + 1) * CHUNK, :].rearrange("(p u) n -> p (u n)", u=2)
+
+        nc.vector.memset(w0_plane[:].bitcast(I32), 0)
+        nc.vector.memset(w1_plane[:].bitcast(I32), 0)
+
+        load_x(0, 0, EARLY_CHUNKS)
+        nc.sync.dma_start(
+            out=w0_codes[:].bitcast(I32).rearrange("p (a n) -> p a n", a=PASSES),
+            in_=w0_words.rearrange("a p n -> p a n").bitcast(I32),
+        )
+        for q in range(4):
+            nc.sync.dma_start(
+                out=w0_plane[32 * q : 32 * q + 4, :].bitcast(I32).rearrange("p (a n) -> p a n", a=PASSES),
+                in_=w0_scales[:, 4 * q : 4 * q + 4, :].rearrange("a r n -> r a n").bitcast(I32),
+            )
+        nc.sync.dma_start(out=w1_first[:].bitcast(I32), in_=w1_words[0].rearrange("p n i -> p (n i)").bitcast(I32))
+        load_x(1, 0, EARLY_CHUNKS)
+        for q in range(4):
+            nc.sync.dma_start(
+                out=w1_plane[32 * q + 4 : 32 * q + 16, :].bitcast(I32),
+                in_=w1_scales[:, 4 * q : 4 * q + 4, :].bitcast(I32),
+            )
+        nc.sync.dma_start(
+            out=w1_rest[:].bitcast(I32).rearrange("p (a n) -> p a n", a=PASSES - 1),
+            in_=w1_words[1:PASSES].rearrange("a p n i -> p a (n i)").bitcast(I32),
+        )
+        load_x(2, 0, EARLY_CHUNKS)
+        for a in range(PASSES):
+            load_w2(a)
+
+        open_banks(1, 0)
+        open_banks(0, 4)
+        for a in range(PASSES):
+            round_x("vector", a, 1)
+            round_x("scalar", a, 2)
+            round_x("vector", a, 0)
+            round_x("scalar", a, 3)
+            for c in (1, 0, 2, 3):
+                quantize("x", a, c)
+            mm_block(1, 0, a, start=a == 0)
+            mm_block(0, 0, a, start=a == 0)
+            mm_block(1, 1, a, stop=a == PASSES - 1)
+            mm_block(0, 1, a)
+
+        for a in range(PASSES):
+            load_x(a, EARLY_CHUNKS, X_COLS // CHUNK)
+        for j in range(4):
+            nc.sync.dma_start(out=res[j][:], in_=rows_of(r, j))
+
+        for u, h in BANKS:
+            park(1, u, h)
+
+        open_banks(2, 0)
+        round_w2("vector", 0, 0)
+        round_w2("vector", 0, 1)
+        round_w2("scalar", 0, 3)
+        quantize("w2", 0, 0)
+        round_w2("vector", 0, 2)
+        for c in (1, 2, 3):
+            quantize("w2", 0, c)
+        for a in (1, 2):
+            round_w2("vector", a, 0)
+            round_w2("scalar", a, 1)
+            round_w2("vector", a, 2)
+            round_w2("scalar", a, 3)
+            for c in range(4):
+                quantize("w2", a, c)
+        mm_bank(2, 0, 0, (0, 1), start=True)
+        mm_bank(2, 1, 0, (0, 1), start=True)
+        mm_block(0, 2, 0)
+        mm_bank(2, 0, 1, (0, 1), start=True)
+        mm_block(0, 2, 1)
+        mm_bank(2, 1, 1, (0, 1), start=True)
+        mm_block(0, 2, 2, stop=True)
+        for u, h in BANKS:
+            park(0, u, h)
+
+        open_banks(1, 4)
+        for u, h in BANKS:
+            mm_bank(1, u, h, (2,), start=True, stop=True)
+        round_x("vector", 0, 4)
+        for a in range(PASSES):
+            round_x("scalar", a, 5)
+        add_bank(partial[1], 1, 0, 0)
+        quantize("x", 0, 4)
+        round_x("vector", 1, 4)
+        add_bank(partial[1], 1, 1, 0)
+        quantize("x", 1, 4)
+        add_bank(partial[1], 1, 0, 1)
+        add_bank(partial[1], 1, 1, 1)
+        round_x("vector", 2, 4)
+        quantize("x", 0, 5)
+        quantize("x", 2, 4)
+        quantize("x", 1, 5)
+        nc.vector.tensor_tensor(out=res[0][:], in0=partial[0][:], in1=res[0][:], op=ADD)
+        quantize("x", 2, 5)
+        nc.vector.tensor_tensor(out=res[1][:], in0=partial[1][:], in1=res[1][:], op=ADD)
+
+        open_banks(3, 4)
+        for u, h in BANKS:
+            mm_bank(3, u, h, (0,), start=True)
+        for u, h in BANKS:
+            mm_bank(2, u, h, (2,), stop=True)
+            add_bank(res[2], 2, u, h)
+        for u, h in ((0, 0), (0, 1), (1, 0), (1, 1)):
+            mm_bank(3, u, h, (1, 2), stop=True)
+            add_bank(res[3], 3, u, h)
+
+        for j in range(3):
+            nc.sync.dma_start(out=rows_of(out, j), in_=res[j][:])
+        for u in range(2):
+            nc.sync.dma_start(out=rows_of(out, 3)[:, u * M : (u + 1) * M], in_=res[3][:, u * M : (u + 1) * M])

@@ -29,7 +29,7 @@ def tile_mix_dconv_tm_res_kernel(tc, x, w0_words, w0_scales, w1_words, w1_scales
     nc = tc.nc
     with ExitStack() as ctx:
         keep = ctx.enter_context(tc.tile_pool(name="keep", bufs=1))
-        raw_pool = ctx.enter_context(tc.tile_pool(name="raw", bufs=6))
+        raw_pool = ctx.enter_context(tc.tile_pool(name="raw", bufs=5))
         stage = ctx.enter_context(tc.tile_pool(name="stage", bufs=6))
         psum = ctx.enter_context(tc.psum_pool(name="psum", bufs=1))
         ctx.enter_context(tc.manual_schedule())
@@ -38,13 +38,14 @@ def tile_mix_dconv_tm_res_kernel(tc, x, w0_words, w0_scales, w1_words, w1_scales
         x_scales = [keep.tile([P, X_COLS], U8, name="x_scales%d" % a, align_bytes=256) for a in range(PASSES)]
         w2_codes = [keep.tile([P, M], U32, name="w2_codes%d" % a, align_bytes=256) for a in range(PASSES)]
         w2_scales = [keep.tile([P, M], U8, name="w2_scales%d" % a, align_bytes=256) for a in range(PASSES)]
-        w0_codes = keep.tile([P, PASSES * 2 * M], U8, align_bytes=256)
+        w0_first = keep.tile([P, 2 * M], U8, align_bytes=256)
+        w0_rest = keep.tile([P, (PASSES - 1) * 2 * M], U8, align_bytes=256)
+        w0_codes = [w0_first[:], w0_rest[:, 0 : 2 * M], w0_rest[:, 2 * M : 4 * M]]
         w0_plane = keep.tile([P, PASSES * M], U8, align_bytes=256)
-        w1_first = keep.tile([P, M], U32, align_bytes=256)
-        w1_rest = keep.tile([P, (PASSES - 1) * M], U32, align_bytes=256)
+        w1_codes = [keep.tile([P, M], U32, name="w1_codes%d" % a, align_bytes=256) for a in range(PASSES)]
         w1_plane = keep.tile([P, M], U8, align_bytes=256)
         res = [keep.tile([P, 2 * M], F32, name="res%d" % j) for j in range(4)]
-        partial = [keep.tile([P, 2 * M], F32, name="partial%d" % j) for j in range(2)]
+        partial = [keep.tile([P, 2 * M], F32, name="partial%d" % j) for j in range(3)]
 
         x_raw = {}
         w2_raw = {}
@@ -52,7 +53,10 @@ def tile_mix_dconv_tm_res_kernel(tc, x, w0_words, w0_scales, w1_words, w1_scales
         acc = {}
 
         def load_x(a, c0, c1):
-            raw = raw_pool.tile([P, PACK, (c1 - c0) * CHUNK], F32, name="raw", tag="raw")
+            if a == 0:
+                raw = keep.tile([P, PACK, X_COLS], F32, name="x_first")
+            else:
+                raw = raw_pool.tile([P, PACK, (c1 - c0) * CHUNK], F32, name="raw", tag="raw")
             rows = x[a * K_PASS : (a + 1) * K_PASS, c0 * CHUNK : c1 * CHUNK]
             nc.sync.dma_start(out=raw[:], in_=rows.rearrange("(p i) w -> p i w", i=PACK))
             for c in range(c0, c1):
@@ -96,20 +100,39 @@ def tile_mix_dconv_tm_res_kernel(tc, x, w0_words, w0_scales, w1_words, w1_scales
                 out=codes[a][:, cols].bitcast(FP8X4), scales=scales[a][:, cols], in_=staged[(name, a, c)][:]
             )
 
-        def open_banks(j, first_bank):
-            for b, (u, h) in enumerate(BANKS):
-                tag = "bank%d" % (first_bank + b)
+        def open_half(j, h, group):
+            for u in range(2):
+                tag = "bank%d" % (4 * group + 2 * h + u)
                 acc[(j, u, h)] = psum.tile([P, N_TILE], F32, name=tag, tag=tag)
+
+        def mm_half(j, h, steps, start=False, stop=False):
+            for s, (tap, a) in enumerate(steps):
+                for u in range(2):
+                    mm(j, u, h, tap, a, start and s == 0, stop and s == len(steps) - 1)
+
+        def mm_each(j, h, steps, start=False, stop=False):
+            for u in range(2):
+                for s, (tap, a) in enumerate(steps):
+                    mm(j, u, h, tap, a, start and s == 0, stop and s == len(steps) - 1)
+
+        def park_half(j, h):
+            for u in range(2):
+                park(j, u, h)
+
+        def add_rows(j):
+            nc.vector.tensor_tensor(out=res[j][:], in0=partial[j][:], in1=res[j][:], op=ADD)
+
+        def all_passes(*taps):
+            return [(tap, a) for tap in taps for a in range(PASSES)]
 
         def mm(j, u, h, tap, a, start=False, stop=False):
             t0 = (j + tap) * CHUNK + u * P
             n0 = h * N_TILE
             if tap == 0:
-                rhs = w0_codes[:, 2 * (a * M + n0) : 2 * (a * M + n0 + N_TILE)].bitcast(FP4X4)
+                rhs = w0_codes[a][:, 2 * n0 : 2 * (n0 + N_TILE)].bitcast(FP4X4)
                 rhs_scale = w0_plane[:, a * M + n0 : a * M + n0 + N_TILE]
             elif tap == 1:
-                words = w1_first[:, n0 : n0 + N_TILE] if a == 0 else w1_rest[:, (a - 1) * M + n0 : (a - 1) * M + n0 + N_TILE]
-                rhs = words.bitcast(FP8X4)
+                rhs = w1_codes[a][:, n0 : n0 + N_TILE].bitcast(FP8X4)
                 rhs_scale = w1_plane[4 * (a + 1) : P, n0 : n0 + N_TILE]
             else:
                 rhs = w2_codes[a][:, n0 : n0 + N_TILE].bitcast(FP8X4)
@@ -146,113 +169,147 @@ def tile_mix_dconv_tm_res_kernel(tc, x, w0_words, w0_scales, w1_words, w1_scales
         def rows_of(dram, j):
             return dram[j * CHUNK : (j + 1) * CHUNK, :].rearrange("(p u) n -> p (u n)", u=2)
 
-        nc.vector.memset(w0_plane[:].bitcast(I32), 0)
-        nc.vector.memset(w1_plane[:].bitcast(I32), 0)
-
-        load_x(0, 0, EARLY_CHUNKS)
-        nc.sync.dma_start(
-            out=w0_codes[:].bitcast(I32).rearrange("p (a n) -> p a n", a=PASSES),
-            in_=w0_words.rearrange("a p n -> p a n").bitcast(I32),
-        )
-        for q in range(4):
+        def load_w1(a):
             nc.sync.dma_start(
-                out=w0_plane[32 * q : 32 * q + 4, :].bitcast(I32).rearrange("p (a n) -> p a n", a=PASSES),
-                in_=w0_scales[:, 4 * q : 4 * q + 4, :].rearrange("a r n -> r a n").bitcast(I32),
+                out=w1_codes[a][:].bitcast(I32), in_=w1_words[a].rearrange("p n i -> p (n i)").bitcast(I32)
             )
-        nc.sync.dma_start(out=w1_first[:].bitcast(I32), in_=w1_words[0].rearrange("p n i -> p (n i)").bitcast(I32))
-        load_x(1, 0, EARLY_CHUNKS)
-        for q in range(4):
-            nc.sync.dma_start(
-                out=w1_plane[32 * q + 4 : 32 * q + 16, :].bitcast(I32),
-                in_=w1_scales[:, 4 * q : 4 * q + 4, :].bitcast(I32),
-            )
-        nc.sync.dma_start(
-            out=w1_rest[:].bitcast(I32).rearrange("p (a n) -> p a n", a=PASSES - 1),
-            in_=w1_words[1:PASSES].rearrange("a p n i -> p a (n i)").bitcast(I32),
-        )
-        load_x(2, 0, EARLY_CHUNKS)
-        for a in range(PASSES):
-            load_w2(a)
 
-        open_banks(1, 0)
-        open_banks(0, 4)
-        for a in range(PASSES):
+        def prepare_x_early(a):
             round_x("vector", a, 1)
             round_x("scalar", a, 2)
             round_x("vector", a, 0)
             round_x("scalar", a, 3)
             for c in (1, 0, 2, 3):
                 quantize("x", a, c)
-            mm_block(1, 0, a, start=a == 0)
-            mm_block(0, 0, a, start=a == 0)
-            mm_block(1, 1, a, stop=a == PASSES - 1)
-            mm_block(0, 1, a)
 
-        for a in range(PASSES):
-            load_x(a, EARLY_CHUNKS, X_COLS // CHUNK)
-        for j in range(4):
-            nc.sync.dma_start(out=res[j][:], in_=rows_of(r, j))
-
-        for u, h in BANKS:
-            park(1, u, h)
-
-        open_banks(2, 0)
-        round_w2("vector", 0, 0)
-        round_w2("vector", 0, 1)
-        round_w2("scalar", 0, 3)
-        quantize("w2", 0, 0)
-        round_w2("vector", 0, 2)
-        for c in (1, 2, 3):
-            quantize("w2", 0, c)
-        for a in (1, 2):
+        def prepare_w2(a, between):
             round_w2("vector", a, 0)
             round_w2("scalar", a, 1)
             round_w2("vector", a, 2)
+            between()
             round_w2("scalar", a, 3)
             for c in range(4):
                 quantize("w2", a, c)
-        mm_bank(2, 0, 0, (0, 1), start=True)
-        mm_bank(2, 1, 0, (0, 1), start=True)
-        mm_block(0, 2, 0)
-        mm_bank(2, 0, 1, (0, 1), start=True)
-        mm_block(0, 2, 1)
-        mm_bank(2, 1, 1, (0, 1), start=True)
-        mm_block(0, 2, 2, stop=True)
-        for u, h in BANKS:
-            park(0, u, h)
 
-        open_banks(1, 4)
-        for u, h in BANKS:
-            mm_bank(1, u, h, (2,), start=True, stop=True)
-        round_x("vector", 0, 4)
+        nc.vector.memset(w0_plane[:].bitcast(I32), 0)
+        nc.vector.memset(w1_plane[:].bitcast(I32), 0)
+        for q in range(4):
+            nc.gpsimd.dma_start(
+                out=w0_plane[32 * q : 32 * q + 4, :].bitcast(I32).rearrange("p (a n) -> p a n", a=PASSES),
+                in_=w0_scales[:, 4 * q : 4 * q + 4, :].rearrange("a r n -> r a n").bitcast(I32),
+            )
+        for q in range(4):
+            nc.gpsimd.dma_start(
+                out=w1_plane[32 * q + 4 : 32 * q + 16, :].bitcast(I32),
+                in_=w1_scales[:, 4 * q : 4 * q + 4, :].bitcast(I32),
+            )
+        load_x(0, 0, X_COLS // CHUNK)
+        nc.sync.dma_start(out=w0_first[:].bitcast(I32), in_=w0_words[0].bitcast(I32))
+        load_w1(0)
+        load_x(1, 0, EARLY_CHUNKS)
+        load_w1(1)
+        nc.sync.dma_start(
+            out=w0_rest[:].bitcast(I32).rearrange("p (a n) -> p a n", a=PASSES - 1),
+            in_=w0_words[1:PASSES].rearrange("a p n -> p a n").bitcast(I32),
+        )
+        load_x(2, 0, EARLY_CHUNKS)
+        load_w1(2)
         for a in range(PASSES):
-            round_x("scalar", a, 5)
-        add_bank(partial[1], 1, 0, 0)
+            load_w2(a)
+
+        for h in range(2):
+            open_half(1, h, 0)
+            open_half(0, h, 1)
+        prepare_x_early(0)
+        round_x("vector", 0, 4)
+        round_x("scalar", 0, 5)
         quantize("x", 0, 4)
-        round_x("vector", 1, 4)
-        add_bank(partial[1], 1, 1, 0)
-        quantize("x", 1, 4)
-        add_bank(partial[1], 1, 0, 1)
-        add_bank(partial[1], 1, 1, 1)
-        round_x("vector", 2, 4)
         quantize("x", 0, 5)
+        mm_block(1, 0, 0, start=True)
+        mm_block(0, 0, 0, start=True)
+        mm_block(1, 1, 0)
+        mm_block(0, 1, 0)
+        prepare_x_early(1)
+        mm_block(0, 1, 1)
+        mm_block(1, 1, 1)
+        mm_half(1, 0, [(0, 1)], stop=True)
+        mm_half(1, 1, [(0, 1)])
+        mm_block(0, 0, 1)
+        park_half(1, 0)
+
+        open_half(2, 0, 0)
+        mm_half(2, 0, [(0, 0), (0, 1), (1, 0), (1, 1)], start=True)
+        prepare_x_early(2)
+        mm_half(1, 1, [(0, 2)])
+        mm_block(0, 0, 2)
+        mm_half(2, 0, [(0, 2)])
+        mm_half(1, 1, [(1, 2)], stop=True)
+        mm_block(0, 1, 2)
+        mm_half(2, 0, [(1, 2)])
+        park_half(1, 1)
+
+        nc.sync.dma_start(out=res[1][:], in_=rows_of(r, 1))
+        for a in (1, 2):
+            load_x(a, EARLY_CHUNKS, X_COLS // CHUNK)
+        for j in (0, 2, 3):
+            nc.sync.dma_start(out=res[j][:], in_=rows_of(r, j))
+
+        open_half(2, 1, 0)
+        prepare_w2(0, lambda: None)
+        mm_bank(2, 0, 1, (0, 1), start=True)
+        mm_half(2, 0, [(2, 0)], stop=True)
+        park_half(2, 0)
+        mm_block(0, 2, 0)
+        mm_bank(2, 1, 1, (0, 1), start=True)
+        mm_half(2, 1, [(2, 0)])
+        open_half(3, 0, 0)
+        mm_each(3, 0, all_passes(0) + [(1, 0), (2, 0)], start=True)
+        prepare_w2(1, lambda: None)
+        mm_block(0, 2, 1)
+        prepare_w2(2, lambda: None)
+        mm_block(0, 2, 2, stop=True)
+        park_half(0, 0)
+        park_half(0, 1)
+
+        open_half(1, 0, 1)
+        open_half(1, 1, 1)
+        mm_each(1, 0, [(0, 2), (1, 2)] + all_passes(2), start=True, stop=True)
+        mm_each(1, 1, all_passes(2), start=True, stop=True)
+        add_rows(1)
+        round_x("vector", 1, 4)
+        round_x("scalar", 1, 5)
+        round_x("scalar", 2, 5)
+        add_bank(res[1], 1, 0, 0)
+        quantize("x", 1, 4)
+        round_x("vector", 2, 4)
+        add_bank(res[1], 1, 1, 0)
         quantize("x", 2, 4)
+        add_bank(res[1], 1, 0, 1)
         quantize("x", 1, 5)
-        nc.vector.tensor_tensor(out=res[0][:], in0=partial[0][:], in1=res[0][:], op=ADD)
+        add_bank(res[1], 1, 1, 1)
         quantize("x", 2, 5)
-        nc.vector.tensor_tensor(out=res[1][:], in0=partial[1][:], in1=res[1][:], op=ADD)
+        add_rows(0)
 
-        open_banks(3, 4)
-        for u, h in BANKS:
-            mm_bank(3, u, h, (0,), start=True)
-        for u, h in BANKS:
-            mm_bank(2, u, h, (2,), stop=True)
-            add_bank(res[2], 2, u, h)
-        for u, h in ((0, 0), (0, 1), (1, 0), (1, 1)):
-            mm_bank(3, u, h, (1, 2), stop=True)
-            add_bank(res[3], 3, u, h)
+        later = [(2, 1), (2, 2)]
+        mm_each(2, 1, later, stop=True)
+        open_half(2, 0, 1)
+        mm_each(2, 0, later, start=True, stop=True)
+        half_of = lambda tile: tile[:].rearrange("p (u n) -> p u n", u=2)[:, :, 0:N_TILE]
+        nc.vector.tensor_tensor(out=half_of(res[2]), in0=half_of(partial[2]), in1=half_of(res[2]), op=ADD)
+        for u in range(2):
+            for h in (1, 0):
+                add_bank(res[2], 2, u, h)
+        open_half(3, 1, 1)
+        for u in range(2):
+            for s, (tap, a) in enumerate([(1, 1), (1, 2), (2, 1), (2, 2)]):
+                mm(3, u, 0, tap, a, stop=s == 3)
+            add_bank(res[3], 3, u, 0)
+            mm_bank(3, u, 1, (0, 1, 2), start=True, stop=True)
+            add_bank(res[3], 3, u, 1)
 
-        for j in range(3):
+        for j in (1, 0):
             nc.sync.dma_start(out=rows_of(out, j), in_=res[j][:])
         for u in range(2):
-            nc.sync.dma_start(out=rows_of(out, 3)[:, u * M : (u + 1) * M], in_=res[3][:, u * M : (u + 1) * M])
+            nc.sync.dma_start(out=rows_of(out, 2)[:, u * M : (u + 1) * M], in_=res[2][:, u * M : (u + 1) * M])
+        for cols in (slice(0, M), cols_of(1, 0), cols_of(1, 1)):
+            nc.sync.dma_start(out=rows_of(out, 3)[:, cols], in_=res[3][:, cols])

from contextlib import ExitStack

import concourse.mybir as mybir

D, K, M, T = 256, 1536, 1024, 1024
FLOPS = 2 * 3 * K * M * T

F32 = mybir.dt.float32
BF16 = mybir.dt.bfloat16
I32 = mybir.dt.int32
U32 = mybir.dt.uint32
U8 = mybir.dt.uint8
FP8X4 = mybir.dt.float8_e4m3fn_x4
FP4X4 = mybir.dt.float4_e2m1fn_x4
ADD = mybir.AluOpType.add

P = 128
PACK = 4
K_PASS = P * PACK
PASSES = K // K_PASS
CHUNK = D
N_TILE = 512
X_COLS = T + 2 * D
EARLY_CHUNKS = 4
BANKS = [(0, 0), (1, 0), (0, 1), (1, 1)]


def tile_mix_dconv_tm_res_kernel(tc, x, w0_words, w0_scales, w1_words, w1_scales, w2, r, out):
    nc = tc.nc
    with ExitStack() as ctx:
        keep = ctx.enter_context(tc.tile_pool(name="keep", bufs=1))
        raw_pool = ctx.enter_context(tc.tile_pool(name="raw", bufs=5))
        stage = ctx.enter_context(tc.tile_pool(name="stage", bufs=6))
        psum = ctx.enter_context(tc.psum_pool(name="psum", bufs=1))
        ctx.enter_context(tc.manual_schedule())

        x_codes = [keep.tile([P, X_COLS], U32, name="x_codes%d" % a, align_bytes=256) for a in range(PASSES)]
        x_scales = [keep.tile([P, X_COLS], U8, name="x_scales%d" % a, align_bytes=256) for a in range(PASSES)]
        w2_codes = [keep.tile([P, M], U32, name="w2_codes%d" % a, align_bytes=256) for a in range(PASSES)]
        w2_scales = [keep.tile([P, M], U8, name="w2_scales%d" % a, align_bytes=256) for a in range(PASSES)]
        w0_first = keep.tile([P, 2 * M], U8, align_bytes=256)
        w0_rest = keep.tile([P, (PASSES - 1) * 2 * M], U8, align_bytes=256)
        w0_codes = [w0_first[:], w0_rest[:, 0 : 2 * M], w0_rest[:, 2 * M : 4 * M]]
        w0_plane = keep.tile([P, PASSES * M], U8, align_bytes=256)
        w1_codes = [keep.tile([P, M], U32, name="w1_codes%d" % a, align_bytes=256) for a in range(PASSES)]
        w1_plane = keep.tile([P, M], U8, align_bytes=256)
        res = [keep.tile([P, 2 * M], F32, name="res%d" % j) for j in range(4)]
        partial = [keep.tile([P, 2 * M], F32, name="partial%d" % j) for j in range(3)]

        x_raw = {}
        w2_raw = {}
        staged = {}
        acc = {}

        def load_x(a, c0, c1):
            if a == 0:
                raw = keep.tile([P, PACK, X_COLS], F32, name="x_first")
            else:
                raw = raw_pool.tile([P, PACK, (c1 - c0) * CHUNK], F32, name="raw", tag="raw")
            rows = x[a * K_PASS : (a + 1) * K_PASS, c0 * CHUNK : c1 * CHUNK]
            nc.sync.dma_start(out=raw[:], in_=rows.rearrange("(p i) w -> p i w", i=PACK))
            for c in range(c0, c1):
                x_raw[(a, c)] = raw[:, :, (c - c0) * CHUNK : (c - c0 + 1) * CHUNK]

        def load_w2(a):
            raw = raw_pool.tile([P, PACK, M], F32, name="raw", tag="raw")
            rows = w2[a * K_PASS : (a + 1) * K_PASS, :]
            nc.sync.dma_start(out=raw[:], in_=rows.rearrange("(p i) w -> p i w", i=PACK))
            for c in range(M // CHUNK):
                w2_raw[(a, c)] = raw[:, :, c * CHUNK : (c + 1) * CHUNK]

        def copy_on(engine, dst, src):
            if engine == "vector":
                nc.vector.tensor_copy(out=dst, in_=src)
            else:
                nc.scalar.copy(out=dst, in_=src)

        def round_x(engine, a, c):
            grouped = stage.tile([P, PACK * CHUNK], BF16, name="grouped", tag="grouped", align_bytes=256)
            copy_on(
                engine,
                grouped[:].rearrange("p (u g e i) -> p g i u e", u=2, e=2, i=PACK),
                x_raw[(a, c)].rearrange("p i (g e u) -> p g i u e", e=2, u=2),
            )
            staged[("x", a, c)] = grouped

        def round_w2(engine, a, c):
            grouped = stage.tile([P, PACK * CHUNK], BF16, name="grouped", tag="grouped", align_bytes=256)
            copy_on(
                engine,
                grouped[:].rearrange("p (g e i) -> p g i e", e=4, i=PACK),
                w2_raw[(a, c)].rearrange("p i (g e) -> p g i e", e=4),
            )
            staged[("w2", a, c)] = grouped

        def quantize(name, a, c):
            codes, scales = (x_codes, x_scales) if name == "x" else (w2_codes, w2_scales)
            cols = slice(c * CHUNK, (c + 1) * CHUNK)
            nc.vector.quantize_mx(
                out=codes[a][:, cols].bitcast(FP8X4), scales=scales[a][:, cols], in_=staged[(name, a, c)][:]
            )

        def open_half(j, h, group):
            for u in range(2):
                tag = "bank%d" % (4 * group + 2 * h + u)
                acc[(j, u, h)] = psum.tile([P, N_TILE], F32, name=tag, tag=tag)

        def mm_half(j, h, steps, start=False, stop=False):
            for s, (tap, a) in enumerate(steps):
                for u in range(2):
                    mm(j, u, h, tap, a, start and s == 0, stop and s == len(steps) - 1)

        def mm_each(j, h, steps, start=False, stop=False):
            for u in range(2):
                for s, (tap, a) in enumerate(steps):
                    mm(j, u, h, tap, a, start and s == 0, stop and s == len(steps) - 1)

        def park_half(j, h):
            for u in range(2):
                park(j, u, h)

        def add_rows(j):
            nc.vector.tensor_tensor(out=res[j][:], in0=partial[j][:], in1=res[j][:], op=ADD)

        def all_passes(*taps):
            return [(tap, a) for tap in taps for a in range(PASSES)]

        def mm(j, u, h, tap, a, start=False, stop=False):
            t0 = (j + tap) * CHUNK + u * P
            n0 = h * N_TILE
            if tap == 0:
                rhs = w0_codes[a][:, 2 * n0 : 2 * (n0 + N_TILE)].bitcast(FP4X4)
                rhs_scale = w0_plane[:, a * M + n0 : a * M + n0 + N_TILE]
            elif tap == 1:
                rhs = w1_codes[a][:, n0 : n0 + N_TILE].bitcast(FP8X4)
                rhs_scale = w1_plane[4 * (a + 1) : P, n0 : n0 + N_TILE]
            else:
                rhs = w2_codes[a][:, n0 : n0 + N_TILE].bitcast(FP8X4)
                rhs_scale = w2_scales[a][:, n0 : n0 + N_TILE]
            nc.tensor.matmul_mx(
                out=acc[(j, u, h)][:],
                lhsT=x_codes[a][:, t0 : t0 + P].bitcast(FP8X4),
                lhsT_scale=x_scales[a][:, t0 : t0 + P],
                rhs=rhs,
                rhs_scale=rhs_scale,
                start=start,
                stop=stop,
            )

        def mm_block(j, tap, a, start=False, stop=False):
            for u, h in BANKS:
                mm(j, u, h, tap, a, start, stop)

        def mm_bank(j, u, h, taps, start=False, stop=False):
            steps = [(tap, a) for tap in taps for a in range(PASSES)]
            for s, (tap, a) in enumerate(steps):
                mm(j, u, h, tap, a, start and s == 0, stop and s == len(steps) - 1)

        def cols_of(u, h):
            return slice(u * M + h * N_TILE, u * M + (h + 1) * N_TILE)

        def park(j, u, h):
            nc.scalar.copy(out=partial[j][:, cols_of(u, h)], in_=acc[(j, u, h)][:])

        def add_bank(dst, j, u, h):
            view = dst[:, cols_of(u, h)]
            nc.vector.tensor_tensor(out=view, in0=acc[(j, u, h)][:], in1=view, op=ADD)

        def rows_of(dram, j):
            return dram[j * CHUNK : (j + 1) * CHUNK, :].rearrange("(p u) n -> p (u n)", u=2)

        def load_w1(a):
            nc.sync.dma_start(
                out=w1_codes[a][:].bitcast(I32), in_=w1_words[a].rearrange("p n i -> p (n i)").bitcast(I32)
            )

        def prepare_x_early(a):
            round_x("vector", a, 1)
            round_x("scalar", a, 2)
            round_x("vector", a, 0)
            round_x("scalar", a, 3)
            for c in (1, 0, 2, 3):
                quantize("x", a, c)

        def prepare_w2(a, between):
            round_w2("vector", a, 0)
            round_w2("scalar", a, 1)
            round_w2("vector", a, 2)
            between()
            round_w2("scalar", a, 3)
            for c in range(4):
                quantize("w2", a, c)

        nc.vector.memset(w0_plane[:].bitcast(I32), 0)
        nc.vector.memset(w1_plane[:].bitcast(I32), 0)
        for q in range(4):
            nc.gpsimd.dma_start(
                out=w0_plane[32 * q : 32 * q + 4, :].bitcast(I32).rearrange("p (a n) -> p a n", a=PASSES),
                in_=w0_scales[:, 4 * q : 4 * q + 4, :].rearrange("a r n -> r a n").bitcast(I32),
            )
        for q in range(4):
            nc.gpsimd.dma_start(
                out=w1_plane[32 * q + 4 : 32 * q + 16, :].bitcast(I32),
                in_=w1_scales[:, 4 * q : 4 * q + 4, :].bitcast(I32),
            )
        load_x(0, 0, X_COLS // CHUNK)
        nc.sync.dma_start(out=w0_first[:].bitcast(I32), in_=w0_words[0].bitcast(I32))
        load_w1(0)
        load_x(1, 0, EARLY_CHUNKS)
        load_w1(1)
        nc.sync.dma_start(
            out=w0_rest[:].bitcast(I32).rearrange("p (a n) -> p a n", a=PASSES - 1),
            in_=w0_words[1:PASSES].rearrange("a p n -> p a n").bitcast(I32),
        )
        load_x(2, 0, EARLY_CHUNKS)
        load_w1(2)
        for a in range(PASSES):
            load_w2(a)

        for h in range(2):
            open_half(1, h, 0)
            open_half(0, h, 1)
        prepare_x_early(0)
        round_x("vector", 0, 4)
        round_x("scalar", 0, 5)
        quantize("x", 0, 4)
        quantize("x", 0, 5)
        mm_block(1, 0, 0, start=True)
        mm_block(0, 0, 0, start=True)
        mm_block(1, 1, 0)
        mm_block(0, 1, 0)
        prepare_x_early(1)
        mm_block(0, 1, 1)
        mm_block(1, 1, 1)
        mm_half(1, 0, [(0, 1)], stop=True)
        mm_half(1, 1, [(0, 1)])
        mm_block(0, 0, 1)
        park_half(1, 0)

        open_half(2, 0, 0)
        mm_half(2, 0, [(0, 0), (0, 1), (1, 0), (1, 1)], start=True)
        prepare_x_early(2)
        mm_half(1, 1, [(0, 2)])
        mm_block(0, 0, 2)
        mm_half(2, 0, [(0, 2)])
        mm_half(1, 1, [(1, 2)], stop=True)
        mm_block(0, 1, 2)
        mm_half(2, 0, [(1, 2)])
        park_half(1, 1)

        nc.sync.dma_start(out=res[1][:], in_=rows_of(r, 1))
        for a in (1, 2):
            load_x(a, EARLY_CHUNKS, X_COLS // CHUNK)
        for j in (0, 2, 3):
            nc.sync.dma_start(out=res[j][:], in_=rows_of(r, j))

        open_half(2, 1, 0)
        prepare_w2(0, lambda: None)
        mm_bank(2, 0, 1, (0, 1), start=True)
        mm_half(2, 0, [(2, 0)], stop=True)
        park_half(2, 0)
        mm_block(0, 2, 0)
        mm_bank(2, 1, 1, (0, 1), start=True)
        mm_half(2, 1, [(2, 0)])
        open_half(3, 0, 0)
        mm_each(3, 0, all_passes(0) + [(1, 0), (2, 0)], start=True)
        prepare_w2(1, lambda: None)
        mm_block(0, 2, 1)
        prepare_w2(2, lambda: None)
        mm_block(0, 2, 2, stop=True)
        park_half(0, 0)
        park_half(0, 1)

        open_half(1, 0, 1)
        open_half(1, 1, 1)
        mm_each(1, 0, [(0, 2), (1, 2)] + all_passes(2), start=True, stop=True)
        mm_each(1, 1, all_passes(2), start=True, stop=True)
        add_rows(1)
        round_x("vector", 1, 4)
        round_x("scalar", 1, 5)
        round_x("scalar", 2, 5)
        add_bank(res[1], 1, 0, 0)
        quantize("x", 1, 4)
        round_x("vector", 2, 4)
        add_bank(res[1], 1, 1, 0)
        quantize("x", 2, 4)
        add_bank(res[1], 1, 0, 1)
        quantize("x", 1, 5)
        add_bank(res[1], 1, 1, 1)
        quantize("x", 2, 5)
        add_rows(0)

        later = [(2, 1), (2, 2)]
        mm_each(2, 1, later, stop=True)
        open_half(2, 0, 1)
        mm_each(2, 0, later, start=True, stop=True)
        half_of = lambda tile: tile[:].rearrange("p (u n) -> p u n", u=2)[:, :, 0:N_TILE]
        nc.vector.tensor_tensor(out=half_of(res[2]), in0=half_of(partial[2]), in1=half_of(res[2]), op=ADD)
        for u in range(2):
            for h in (1, 0):
                add_bank(res[2], 2, u, h)
        open_half(3, 1, 1)
        for u in range(2):
            for s, (tap, a) in enumerate([(1, 1), (1, 2), (2, 1), (2, 2)]):
                mm(3, u, 0, tap, a, stop=s == 3)
            add_bank(res[3], 3, u, 0)
            mm_bank(3, u, 1, (0, 1, 2), start=True, stop=True)
            add_bank(res[3], 3, u, 1)

        for j in (1, 0):
            nc.sync.dma_start(out=rows_of(out, j), in_=res[j][:])
        for u in range(2):
            nc.sync.dma_start(out=rows_of(out, 2)[:, u * M : (u + 1) * M], in_=res[2][:, u * M : (u + 1) * M])
        for cols in (slice(0, M), cols_of(1, 0), cols_of(1, 1)):
            nc.sync.dma_start(out=rows_of(out, 3)[:, cols], in_=res[3][:, cols])
